import numpy as np, ml_dtypes
CORES = [3,11,19,27,35,43]
N = 6
import mx_ref
BF = ml_dtypes.bfloat16
def cols(t, e):
    v = np.concatenate([t.reshape(128, -1, 4), np.zeros((128, 1, 4), BF)], axis=1)
    return np.ascontiguousarray(v[:, e]).reshape(128, -1)
def f(rng, *shape):
    return mx_ref.flush((rng.standard_normal(shape, dtype=np.float32) * np.exp2(rng.integers(-2, 3, shape[:-1] + (1,)))).astype(BF))
def wide(rng, *shape, cols=0):
    v = rng.standard_normal(shape, dtype=np.float32) * np.exp2(rng.integers(-12, 13, shape)).astype(np.float32)
    if cols: v *= np.repeat(np.exp2(rng.integers(-cols, cols + 1, shape[:-2] + (1, shape[-1] // 4))) * (rng.random(shape[:-2] + (1, shape[-1] // 4)) > 0.0625), 4, axis=-1).astype(np.float32)
    return mx_ref.flush(v.astype(BF))
T, NBIT, K, O = 160, 8, 256, 3
def planes(rng):
    v = np.zeros((N, 128, 512), BF); v[:, :, :4 * NBIT] = f(rng, N, 128, 4 * NBIT); return v
def setup_inputs(rng):
    return {"x": f(rng, N, 128, 4 * T), "hp": planes(rng), "e": f(rng, N, 128, 4 * K), "qw": f(rng, N, 128, O * 512)}
def setup_inputs_zero(rng):
    d = setup_inputs(rng)
    for r in rng.permutation(N)[:N // 2]:
        i = rng.integers(0, NBIT); d["hp"][r, :, 4 * i:4 * i + 4] = 0
    for r in range(N):
        for j in rng.permutation(T)[:T // 8]: d["x"][r, :, 4 * j:4 * j + 4] = 0
    return d
def setup_inputs_onebucket(rng):
    d = setup_inputs(rng); d["x"] = np.tile(d["hp"][rng.integers(0, N)][:, :4], (N, 1, T)); return d
def setup_inputs_all(rng):
    d = setup_inputs(rng); g = f(rng, 128, 4).astype(np.float32)[None, :, None, :]
    d["hp"][:, :, :4 * NBIT] = (g * np.exp2(rng.integers(0, 4, (N, 1, NBIT, 1)))).reshape(N, 128, -1).astype(BF)
    s = np.stack([rng.permutation(T) % 2 * 2 - 1 for r in range(N)]) * np.exp2(rng.integers(0, 4, (N, T)))
    d["x"] = (g * s[:, None, :, None]).reshape(N, 128, -1).astype(BF); return d
def setup_inputs_small(rng):
    d = setup_inputs(rng)
    for k in ("x", "hp"):
        v = d[k].astype(np.float32) * np.float32(2.0 ** -24)
        d[k] = mx_ref.flush(np.where(np.abs(v) < np.float32(2.0 ** -30), np.float32(0), v).astype(BF))
    return d
def setup_inputs_spread(rng):
    d = setup_inputs(rng); d["x"] = wide(rng, N, 128, 4 * T, cols=8); d["e"] = wide(rng, N, 128, 4 * K, cols=8); return d
def check_inputs(d):
    b = []
    if (np.asarray(d["hp"]).astype(np.float32)[:, :, 4 * NBIT:] != 0).any(): b.append("hp")
    return b
def reference(x, hp, e, qw):
    X = [mx_ref.quantize(x[r]) for r in range(N)]
    H = [mx_ref.quantize(hp[q]) for q in range(N)]
    W = [[mx_ref.quantize(np.ascontiguousarray(qw[r][:, 512 * o:512 * o + 512])) for o in range(O)] for r in range(N)]
    y = np.zeros((N, 128, N * O * T), np.float32); bk = np.zeros((N, N, T), np.float32)
    for r in range(N):
        for q in range(N):
            s = mx_ref.matmul(H[q], X[r])
            b = np.zeros(T, int)
            for i in range(NBIT): b += 2 ** i * (s[i] > 0)
            bk[r, q] = b
            c = mx_ref.quantize(cols(e[q], b))
            for o in range(O):
                k = (q * O + o) * T
                y[r][:, k:k + T] = mx_ref.matmul(W[r][o], c)
    return {"y": y, "bk": bk}

@@ -1,0 +1,319 @@
+from concourse.bass import DstId, RemoteDMATransfer
+from concourse.mybir import dt, AluOpType, ActivationFunctionType
+
+N, TOK, NBIT, K, O = 6, 160, 8, 256, 3
+NC = TOK // 16
+NR = NBIT * (N - 1)
+A0 = 128
+GAP = A0 + NR
+Z1 = GAP + NBIT
+ZL = 120
+GROUPS = ((0, 3), (3, 6), (6, 9), (9, 10))
+BANKS = 8
+SPLIT_LAST = True
+
+SCRATCH = {
+    "hpt": ("sbuf", [128, 4 * (ZL + 128)], "bfloat16"),
+    "zt": ("sbuf", [128, 512], "bfloat16"),
+    "et": ("sbuf", [128, 4 * K], "bfloat16"),
+    "xs": ("sbuf", [128, NC, 64], "bfloat16"),
+    "xrep": ("sbuf", [128, NC, 512], "bfloat16"),
+    "qwt": ("sbuf", [128, O * 512], "bfloat16"),
+    "hq": ("sbuf", [128, 128], "float8_e4m3fn_x4"),
+    "hqz": ("sbuf", [128, 128], "uint8"),
+    "pc": ("sbuf", [128, Z1 + 128], "float8_e4m3fn_x4"),
+    "pz": ("sbuf", [128, Z1 + 128], "uint8"),
+    "oc": ("sbuf", [128, ZL + 128], "float8_e4m3fn_x4"),
+    "oz": ("sbuf", [128, ZL + 128], "uint8"),
+    "ec": ("sbuf", [128, K], "float8_e4m3fn_x4"),
+    "ez": ("sbuf", [128, K], "uint8"),
+    "hc": ("sbuf", [128, K], "float8_e4m3fn_x4"),
+    "hz": ("sbuf", [128, K], "uint8"),
+    "xc": ("sbuf", [128, NC * 128], "float8_e4m3fn_x4"),
+    "xz": ("sbuf", [128, NC * 128], "uint8"),
+    "wc": ("sbuf", [128, O * 128], "float8_e4m3fn_x4"),
+    "wz": ("sbuf", [128, O * 128], "uint8"),
+    "coef": ("sbuf", [128, 3 * NR], "float32"),
+    "obits": ("sbuf", [128, NC * NBIT], "float32"),
+    "osc": ("sbuf", [128, NC * NBIT], "float32"),
+    "bits": ("sbuf", [128, NC * NR], "float32"),
+    "sc": ("sbuf", [128, NC * NR], "float32"),
+    "li": ("sbuf", [128, NC * N], "uint16"),
+    "bf": ("sbuf", [128, 64], "float32"),
+    "bt": ("sbuf", [128, 64], "float32"),
+    "pr": ("sbuf", [128, N * O * K], "float32"),
+    "yo": ("sbuf", [128, N * O * TOK], "float32"),
+}
+for _j in range(N - 1):
+    SCRATCH["tc%d" % _j] = ("sbuf", [128, K], "float8_e4m3fn_x4")
+    SCRATCH["tz%d" % _j] = ("sbuf", [128, K], "uint8")
+for _j in range(BANKS):
+    SCRATCH["pb%d" % _j] = ("psum", [128, 512], "float32")
+
+SEMAPHORES = ["lde", "ldh", "ldx", "ldw", "gap", "sv", "ss", "st", "ls", "hpl", "hzs", "hcs", "pls", "yst"] + ["tb%d" % j for j in range(N)]
+
+
+def bits_of(engines):
+    return sum(1 << e for e in engines)
+
+
+def roads(R, T, topo):
+    me = T.rank_of(R)
+    far = sorted((c for c in T.cores if c != R), key=lambda c: (T.rank_of(c) - me) % N)
+    plane = [c for c in far if topo.same_plane(topo.chip(R), topo.chip(c))]
+    mate = [c for c in far if topo.mates(topo.chip(R), topo.chip(c))]
+    diag = [c for c in far if c not in plane and c not in mate]
+    others = [c for c in topo.cores_of(R) if c != R]
+    owners = [c for c in others if all(topo.may_write(c, d) for d in far)]
+    c1 = [c for c in owners if topo.die(c) == topo.die(R)][0]
+    c2 = [c for c in owners if topo.die(c) != topo.die(R)][0]
+    ha, hb = [c for c in others if c not in owners and topo.die(c) != topo.die(R)][:2]
+    return diag + mate + plane, c1, c2, ha, hb
+
+
+def dst(c, topo):
+    rid, pid, _ = topo.addr(c)
+    return DstId(rid=rid, pnc=pid)
+
+
+def copy_to(cores, src, dsts, mask, sem, topo):
+    return RemoteDMATransfer(dst_ids=[dst(c, topo) for c in cores], dma_engine_mask=mask, remote_sem=sem, srcs=[src], dsts=dsts)
+
+
+def engine_sets(R, near, far, topo):
+    off = topo.engines(R, far)
+    return off, [e for e in topo.engines(R, near) if e not in off]
+
+
+def helper_program(g, core, R, T, topo):
+    dests, c1, c2, ha, hb = roads(R, T, topo)
+    if core not in (c1, c2, ha, hb):
+        return
+    out = topo.engines(core, dests[-1])
+    mask, ne = bits_of(out), len(out)
+    off, inner = engine_sets(R, core, dests[0], topo)
+    codes = core in (c1, ha)
+    mine = [0, 1, 2] if core in (c1, c2) else [3, 4]
+    g.wait_ge(T.sem.hpl, len(off) if codes else len(inner))
+    if codes:
+        src = T.hq[:, 0:NBIT].bitcast(dt.uint8)
+        ds = [T.pc[:, A0 + NBIT * j:A0 + NBIT * (j + 1)].bitcast(dt.uint8) for j in mine]
+    else:
+        src = T.hqz[:, 0:NBIT]
+        ds = [T.pz[:, A0 + NBIT * j:A0 + NBIT * (j + 1)] for j in mine]
+    g.remote_dma_fused([copy_to([dests[j] for j in mine], src, ds, mask, T.sem.pls, topo)], local_sem=T.sem.ls)
+    total = ne
+    if core in (ha, hb):
+        j = 3 if core == ha else 4
+        sem = T.sem["tb%d" % T.rank_of(R)]
+        rid, pid, _ = topo.addr(dests[j])
+        g.wait_ge(T.sem.hzs, len(inner))
+        g.remote_dma(T["tz%d" % j][:, 0:K], T.hz[:, 0:K], sem, T.sem.ls, pid, rid, mask)
+        g.wait_ge(T.sem.hcs, len(inner))
+        g.remote_dma(T["tc%d" % j][:, 0:K].bitcast(dt.uint8), T.hc[:, 0:K].bitcast(dt.uint8), sem, T.sem.ls, pid, rid, mask)
+        total += 2 * ne
+    g.wait_ge(T.sem.ls, total)
+
+
+def rank_program(g, core, T, topo):
+    rank = T.rank_of(core)
+    if rank is None:
+        for R in T.cores:
+            if topo.chip(R) == topo.chip(core):
+                helper_program(g, core, R, T, topo)
+        return
+    dests, c1, c2, ha, hb = roads(core, T, topo)
+    slot_q = [[T.rank_of(c) for c in T.cores if c != core and roads(c, T, topo)[0][j] == core][0] for j in range(N - 1)] + [rank]
+    off, inner = engine_sets(core, ha, dests[0], topo)
+
+    queue = {"v": g.vector, "s": g.scalar, "t": g.tensor, "y": g.sync, "g": g}
+    own_sem = {"v": "sv", "s": "ss", "t": "st"}
+    count = {"v": 0, "s": 0, "t": 0}
+    seen = {}
+
+    def need(q, sem, val):
+        if seen.get((q, sem), 0) < val:
+            seen[(q, sem)] = val
+            queue[q].wait_ge(T.sem[sem], val)
+
+    def done(q, ins):
+        ins.then_inc(T.sem[own_sem[q]], 1)
+        count[q] += 1
+        return (own_sem[q], count[q])
+
+    COPY = ActivationFunctionType.Copy
+
+    def move(q, out, in_, after):
+        for s, v in after:
+            need(q, s, v)
+        if q == "v":
+            return done("v", g.vector.tensor_copy(out, in_))
+        return done("s", g.scalar.activation(out, in_, COPY))
+
+    def quantise(out, scales, in_, after):
+        for s, v in after:
+            need("v", s, v)
+        return done("v", g.vector.quantize_mx(out, scales, in_))
+
+    g.sync.dma_start(T.hpt[:, 4 * ZL:4 * (ZL + NBIT)], T.hp[:, 0:4 * NBIT]).then_inc(T.sem.ldh, 16)
+    g.sync.dma_start(T.et[:, :], T.e[:, :]).then_inc(T.sem.lde, 16)
+    g.sync.dma_start(T.xs[:, :, :], T.x[:, :]).then_inc(T.sem.ldx, 16)
+    g.sync.dma_start(T.qwt[:, :], T.qw[:, :]).then_inc(T.sem.ldw, 16)
+
+    z = done("v", g.vector.memset(T.hpt[:, 4 * (ZL + NBIT):4 * (ZL + 128)], 0.0))
+    half = done("v", g.vector.memset(T.coef[:, :], 0.5))
+    b0 = done("v", g.vector.memset(T.bf[:, :], 0.0))
+    done("v", g.vector.memset(T.hpt[:, 0:4 * ZL], 0.0))
+    zz = done("v", g.vector.memset(T.zt[:, :], 0.0))
+    qh = quantise(T.hq[:, :], T.hqz[:, :], T.hpt[:, 4 * ZL:4 * (ZL + 128)], [("ldh", 16), z])
+    quantise(T.pc[:, 0:A0], T.pz[:, 0:A0], T.zt[:, :], [zz])
+    quantise(T.pc[:, Z1:Z1 + 128], T.pz[:, Z1:Z1 + 128], T.zt[:, :], [])
+    quantise(T.oc[:, :], T.oz[:, :], T.hpt[:, :], [])
+    half = done("v", g.vector.memset(T.coef[:, 0:3 * NR:NBIT], 0.0))
+    qe = quantise(T.ec[:, :], T.ez[:, :], T.et[:, :], [("lde", 16)])
+    cp = []
+    for k in range(8):
+        cp.append(move("s" if k < 3 else "v", T.xrep[:, :, 64 * k:64 * k + 64], T.xs[:, :, :], [("ldx", 16)]))
+    qw = quantise(T.wc[:, :], T.wz[:, :], T.qwt[:, :], [("ldw", 16)])
+    qx = [quantise(T.xc[:, 128 * i:128 * i + 128], T.xz[:, 128 * i:128 * i + 128], T.xrep[:, i, :], [cp[2], cp[7]]) for i in range(NC)]
+    need("y", *qh)
+    g.sync.dma_start(T.pc[:, GAP:Z1].bitcast(dt.uint8), T.hq[:, NBIT:2 * NBIT].bitcast(dt.uint8)).then_inc(T.sem.gap, 16)
+    g.sync.dma_start(T.pz[:, GAP:Z1], T.hqz[:, NBIT:2 * NBIT]).then_inc(T.sem.gap, 16)
+
+    need("g", *qh)
+    pl = T.hq[:, 0:NBIT].bitcast(dt.uint8)
+    g.remote_dma_fused([copy_to([c1, ha], pl, [pl, pl], bits_of(off), T.sem.hpl, topo)], local_sem=T.sem.ls)
+    pl = T.hqz[:, 0:NBIT]
+    g.remote_dma_fused([copy_to([c2, hb], pl, [pl, pl], bits_of(inner), T.sem.hpl, topo)], local_sem=T.sem.ls)
+    need("g", *qe)
+    total = len(off) + len(inner)
+    for src, far, near, sem, codes in ((T.ez[:, 0:K], "tz", T.hz[:, 0:K], T.sem.hzs, False), (T.ec[:, 0:K], "tc", T.hc[:, 0:K], T.sem.hcs, True)):
+        fars = [T["%s%d" % (far, j)][:, 0:K] for j in range(3)]
+        if codes:
+            src, near, fars = src.bitcast(dt.uint8), near.bitcast(dt.uint8), [d.bitcast(dt.uint8) for d in fars]
+        g.remote_dma_fused([copy_to(dests[:3], src, fars, bits_of(off), T.sem["tb%d" % rank], topo),
+                            copy_to([ha, hb], src, [near, near], bits_of(inner), sem, topo)], local_sem=T.sem.ls)
+        total += len(off) + len(inner)
+
+    free = [None] * BANKS
+    unit = [0]
+
+    def bank():
+        b = unit[0] % BANKS
+        unit[0] += 1
+        if free[b] is not None:
+            need("t", *free[b])
+        return b
+
+    def products(cd, sc_, after):
+        res = []
+        for s, v in after:
+            need("t", s, v)
+        for o in range(O):
+            b = bank()
+            m = done("t", g.tensor.matmul_mx(T["pb%d" % b][:, 0:K], T.wc[:, 128 * o:128 * o + 128], T.wz[:, 128 * o:128 * o + 128],
+                                             cd[:, 0:K], sc_[:, 0:K], True, True))
+            res.append((b, m))
+        return res
+
+    def drain(q, slot, o, bm):
+        b, m = bm
+        a = (slot * O + o) * K
+        free[b] = move(q, T.pr[:, a:a + K], T["pb%d" % b][:, 0:K], [m])
+        return free[b]
+
+    def pick(q, slot, o, after):
+        r = slot_q[slot]
+        a, y = (slot * O + o) * K, (r * O + o) * TOK
+        return move(q, T.yo[:, y:y + TOK], T.pr[:, a:a + K].indirect(T.li[:, NC * r:NC * r + NC]), after)
+
+    nst = [0]
+
+    def keep(out, in_, after):
+        for s, v in after:
+            need("y", s, v)
+        g.sync.dma_start(out, in_).then_inc(T.sem.yst, 16)
+        nst[0] += 1
+
+    def store(slot, o0, o1, after):
+        y = (slot_q[slot] * O) * TOK
+        keep(T.y[:, y + o0 * TOK:y + o1 * TOK], T.yo[:, y + o0 * TOK:y + o1 * TOK], after)
+
+    def bucket_products(lo, hi, cd, sc_, at, step):
+        b = bank()
+        for i in range(lo, hi):
+            a = at - step * (i - lo)
+            m = done("t", g.tensor.matmul_mx(T["pb%d" % b][:, 0:128], T.xc[:, 128 * i:128 * i + 128], T.xz[:, 128 * i:128 * i + 128],
+                                             cd[:, a:a + 128], sc_[:, a:a + 128], i == lo, i == hi - 1))
+        return b, m
+
+    def numbers(bm, bits, out, n):
+        b, m = bm
+        need("v", *m)
+        free[b] = done("v", g.vector.tensor_scalar(bits, T["pb%d" % b][:, 0:n], 0.0, 128.0, AluOpType.is_gt, AluOpType.mult))
+        need("v", *free[b])
+        need("v", *half)
+        return done("v", g.vector.tensor_tensor_scan(out, T.coef[:, 0:n], bits, 0.0, AluOpType.mult, AluOpType.add))
+
+    own = N - 1
+    bm = products(T.ec, T.ez, [qe, qw])
+    dr = [drain("s", own, o, bm[o]) for o in range(O)]
+    need("t", *qx[-1])
+    s = numbers(bucket_products(0, NC, T.oc, T.oz, ZL, NBIT), T.obits[:, :], T.osc[:, :], NC * NBIT)
+    li = {own: move("v", T.li[:, NC * rank:NC * rank + NC], T.osc[:, NBIT - 1:NC * NBIT:NBIT], [s])}
+    store(own, 0, O, [pick("s", own, o, [dr[o], li[own]]) for o in range(O)])
+
+    need("t", "gap", 32)
+    need("t", "pls", 2 * len(off) * (N - 1))
+    groups = [bucket_products(lo, hi, T.pc, T.pz, A0, NR) for lo, hi in GROUPS]
+    scans = [numbers(groups[k], T.bits[:, NR * lo:NR * hi], T.sc[:, NR * lo:NR * hi], NR * (hi - lo)) for k, (lo, hi) in enumerate(GROUPS)]
+
+    def make_list(slot):
+        r = slot_q[slot]
+        li[slot] = move("v", T.li[:, NC * r:NC * r + NC], T.sc[:, NBIT * slot + NBIT - 1:NC * NR:NR], [scans[-1]])
+
+    pm, dr = {}, {}
+
+    def fetch(slot):
+        pm[slot] = products(T["tc%d" % slot], T["tz%d" % slot], [("tb%d" % slot_q[slot], 2 * len(off))])
+
+    make_list(0)
+    make_list(1)
+    fetch(0)
+    for o in range(O):
+        dr[0, o] = drain("s", 0, o, pm[0][o])
+    last = N - 2
+    for slot in range(N - 1):
+        nxt = slot + 1
+        if nxt <= last:
+            fetch(nxt)
+        p0 = pick("v", slot, 0, [dr[slot, 0], li[slot]])
+        if nxt <= last:
+            dr[nxt, 0] = drain("v", nxt, 0, pm[nxt][0])
+        p1 = pick("s", slot, 1, [dr[slot, 1], li[slot]])
+        if nxt <= last:
+            dr[nxt, 1] = drain("s", nxt, 1, pm[nxt][1])
+        p2 = pick("v", slot, 2, [dr[slot, 2]])
+        if nxt <= last:
+            dr[nxt, 2] = drain("s", nxt, 2, pm[nxt][2])
+        if slot < last:
+            if nxt < last:
+                make_list(nxt + 1)
+            store(slot, 0, O, [p0, p1, p2])
+        else:
+            store(slot, 0, 2, [p0, p1])
+            store(slot, 2, O, [p2])
+
+    need("v", *b0)
+    h = NC * N // 2
+    move("v", T.bf[0:32, 0:h], T.li[0:32, 0:h], [li[N - 2]])
+    f = move("v", T.bf[0:32, 32:32 + h], T.li[0:32, h:2 * h], [])
+    need("v", *f)
+    tr = done("v", g.vector.transpose(T.bt[0:32, :], T.bf[0:32, :]))
+    keep(T.bk[0:N // 2, :], T.bt[0:h, 0:16], [tr])
+    keep(T.bk[N // 2:N, :], T.bt[0:h, 32:48], [])
+
+    need("y", "yst", 16 * nst[0])
+    need("g", "ls", total)
+    for q in ("v", "s", "t"):
+        need("g", own_sem[q], count[q])

@@ -2,45 +2,69 @@ from concourse.bass import DstId, RemoteDMATransfer
 from concourse.mybir import dt, AluOpType, ActivationFunctionType
 
 N, TOK, NBIT, K, O = 6, 160, 8, 256, 3
-NC = TOK // 16
-NR = NBIT * (N - 1)
-A0 = 128
-GAP = A0 + NR
-Z1 = GAP + NBIT
-ZL = 120
-GROUPS = ((0, 3), (3, 6), (6, 9), (9, 10))
+GP = 16
+NC = TOK // GP
+W = 128
+CUT = (0, 5 * K // 8, K)
 BANKS = 8
-SPLIT_LAST = True
+OWN = N - 1
+
+CALLS = ("po01 pia", "zo01 zib", "So0 Sic", "Ao0 Aia", "Bo0 Bib")
+HANDED = {"a": "po234 Ao1234", "b": "zo234 Bo1234", "c": "So1234"}
+
+CUTS = {"o": ([OWN], (0, NC)), "a": ([0, 1], (0, 8, NC)), "b": ([2, 3, 4], (0, 5, NC))}
+
+LOADS = "x w03"
+TENSOR = "go m5 ga m0 gb0 m1 gb1 m2 m3 m4"
+VECTOR = ("x w03 bo0 so01 lo d52 p50 p52 ba0 sa01 ba1 sa12 la bb0 sb01 d12 bb1 p12 sb12 p10 lb d22 k0 p22 k1 d32 p20 p32 "
+          "d42 p30 p42 p40")
+SCALAR = "d51 d50 p51 d01 d00 d02 p01 p00 p02 d11 d10 p11 d21 d20 p21 d31 d30 p31 d41 d40 p41"
+STORES = "503 003 103 k 203 303 413 401"
+
+
+def lay_out():
+    stages, at, sc, off, zeros, gap = {}, W, 0, 0, [0], None
+    for st, (slots, cuts) in CUTS.items():
+        stages[st] = (slots, at, sc, off, cuts)
+        sc, off = sc + NBIT * len(slots) * NC, off + len(slots) + len(slots) % 2
+        if st == "o":
+            at += W
+            continue
+        at += NBIT * len(slots)
+        if len(slots) % 2:
+            gap, at = at, at + NBIT
+        zeros.append(at)
+        at += W
+    return stages, at, zeros, gap
+
+
+STAGES, PC, ZEROS, GAP = lay_out()
+PLACE = [slot for slots, _ in CUTS.values() for slot in slots]
 
 SCRATCH = {
-    "hpt": ("sbuf", [128, 4 * (ZL + 128)], "bfloat16"),
-    "zt": ("sbuf", [128, 512], "bfloat16"),
+    "hpt": ("sbuf", [128, 4 * (NBIT + W)], "bfloat16"),
     "et": ("sbuf", [128, 4 * K], "bfloat16"),
-    "xs": ("sbuf", [128, NC, 64], "bfloat16"),
-    "xrep": ("sbuf", [128, NC, 512], "bfloat16"),
+    "xs": ("sbuf", [128, 4 * TOK], "bfloat16"),
     "qwt": ("sbuf", [128, O * 512], "bfloat16"),
-    "hq": ("sbuf", [128, 128], "float8_e4m3fn_x4"),
-    "hqz": ("sbuf", [128, 128], "uint8"),
-    "pc": ("sbuf", [128, Z1 + 128], "float8_e4m3fn_x4"),
-    "pz": ("sbuf", [128, Z1 + 128], "uint8"),
-    "oc": ("sbuf", [128, ZL + 128], "float8_e4m3fn_x4"),
-    "oz": ("sbuf", [128, ZL + 128], "uint8"),
+    "pc": ("sbuf", [128, PC], "float8_e4m3fn_x4"),
+    "pz": ("sbuf", [128, PC], "uint8"),
     "ec": ("sbuf", [128, K], "float8_e4m3fn_x4"),
     "ez": ("sbuf", [128, K], "uint8"),
-    "hc": ("sbuf", [128, K], "float8_e4m3fn_x4"),
-    "hz": ("sbuf", [128, K], "uint8"),
-    "xc": ("sbuf", [128, NC * 128], "float8_e4m3fn_x4"),
-    "xz": ("sbuf", [128, NC * 128], "uint8"),
-    "wc": ("sbuf", [128, O * 128], "float8_e4m3fn_x4"),
-    "wz": ("sbuf", [128, O * 128], "uint8"),
-    "coef": ("sbuf", [128, 3 * NR], "float32"),
-    "obits": ("sbuf", [128, NC * NBIT], "float32"),
-    "osc": ("sbuf", [128, NC * NBIT], "float32"),
-    "bits": ("sbuf", [128, NC * NR], "float32"),
-    "sc": ("sbuf", [128, NC * NR], "float32"),
-    "li": ("sbuf", [128, NC * N], "uint16"),
-    "bf": ("sbuf", [128, 64], "float32"),
-    "bt": ("sbuf", [128, 64], "float32"),
+    "xc": ("sbuf", [128, TOK + W], "float8_e4m3fn_x4"),
+    "xz": ("sbuf", [128, TOK + W], "uint8"),
+    "wc": ("sbuf", [128, O * W], "float8_e4m3fn_x4"),
+    "wz": ("sbuf", [128, O * W], "uint8"),
+    "probe": ("sbuf", [128, 1024], "float32"),
+    "part": ("sbuf", [128, 2], "int32"),
+    "num": ("sbuf", [128, 16], "float32"),
+    "turn": ("sbuf", [128, 16], "float32"),
+    "off": ("sbuf", [128, 8], "uint16"),
+    "coef": ("sbuf", [128, TOK], "bfloat16"),
+    "bits": ("sbuf", [128, N * NBIT * NC], "bfloat16"),
+    "sc": ("sbuf", [128, N * NBIT * NC], "bfloat16"),
+    "li": ("sbuf", [128, GP * N], "uint16"),
+    "bf": ("sbuf", [128, GP * N], "float32"),
+    "bt": ("sbuf", [128, GP * N], "float32"),
     "pr": ("sbuf", [128, N * O * K], "float32"),
     "yo": ("sbuf", [128, N * O * TOK], "float32"),
 }
@@ -50,7 +74,8 @@ for _j in range(N - 1):
 for _j in range(BANKS):
     SCRATCH["pb%d" % _j] = ("psum", [128, 512], "float32")
 
-SEMAPHORES = ["lde", "ldh", "ldx", "ldw", "gap", "sv", "ss", "st", "ls", "hpl", "hzs", "hcs", "pls", "yst"] + ["tb%d" % j for j in range(N)]
+SEMAPHORES = (["lde", "ldh", "own", "sv", "ss", "st", "sg", "ls", "yst"] + ["f" + w for w in "pzABCS"] + ["ld" + w for w in LOADS.split()]
+              + ["pl" + st for st in CUTS] + ["tb%d" % j for j in range(N)])
 
 
 def bits_of(engines):
@@ -63,56 +88,62 @@ def roads(R, T, topo):
     plane = [c for c in far if topo.same_plane(topo.chip(R), topo.chip(c))]
     mate = [c for c in far if topo.mates(topo.chip(R), topo.chip(c))]
     diag = [c for c in far if c not in plane and c not in mate]
-    others = [c for c in topo.cores_of(R) if c != R]
-    owners = [c for c in others if all(topo.may_write(c, d) for d in far)]
-    c1 = [c for c in owners if topo.die(c) == topo.die(R)][0]
-    c2 = [c for c in owners if topo.die(c) != topo.die(R)][0]
-    ha, hb = [c for c in others if c not in owners and topo.die(c) != topo.die(R)][:2]
-    return diag + mate + plane, c1, c2, ha, hb
+    near = sorted((c for c in topo.cores_of(R) if c != R), key=lambda c: topo.die(c) != topo.die(R))
+    owners = [c for c in near if all(topo.may_write(c, d) for d in far)]
+    return mate + plane + diag, dict(zip("abcdefg", owners + [c for c in near if c not in owners]))
 
 
-def dst(c, topo):
-    rid, pid, _ = topo.addr(c)
-    return DstId(rid=rid, pnc=pid)
+def engine_sets(R, T, topo):
+    dests, helpers = roads(R, T, topo)
+    off, every = topo.engines(R, dests[0]), topo.engines(R, helpers["a"])
+    inner, h = [e for e in every if e not in off], len(off) // 2
+    return {"o": off, "i": inner, "a": every, "l": off[:h], "h": off[h:], "m": inner[:h], "n": inner[h:]}
 
 
-def copy_to(cores, src, dsts, mask, sem, topo):
-    return RemoteDMATransfer(dst_ids=[dst(c, topo) for c in cores], dma_engine_mask=mask, remote_sem=sem, srcs=[src], dsts=dsts)
+def table(T, slot):
+    return (T.ec, T.ez) if slot == OWN else (T["tc%d" % slot], T["tz%d" % slot])
 
 
-def engine_sets(R, near, far, topo):
-    off = topo.engines(R, far)
-    return off, [e for e in topo.engines(R, near) if e not in off]
+def planes(T, at, what):
+    return T.pc[:, at:at + NBIT].bitcast(dt.uint8) if what == "p" else T.pz[:, at:at + NBIT]
+
+
+def stage_of(slot):
+    return [st for st in STAGES if slot in STAGES[st][0]][0]
+
+
+def piece(T, slot, what):
+    if what in "pz":
+        slots, at = STAGES[stage_of(OWN if slot is None else slot)][:2]
+        return planes(T, at + NBIT * slots.index(OWN if slot is None else slot), what)
+    c, z = table(T, OWN if slot is None else slot)
+    lo, hi = {"A": CUT[:2], "B": CUT[1:], "C": (0, K), "S": (0, K)}[what]
+    return z[:, lo:hi] if what == "S" else c[:, lo:hi].bitcast(dt.uint8)
+
+
+def transfer(what, to, engines, R, T, topo):
+    dests, helpers = roads(R, T, topo)
+    src = piece(T, None, what)
+    if to[0] in helpers:
+        cores, outs, sem = [helpers[h] for h in to], [src] * len(to), "f" + what
+    else:
+        cores, outs = [dests[int(j)] for j in to], [piece(T, int(j), what) for j in to]
+        sem = "pl" + stage_of(int(to[0])) if what in "pz" else "tb%d" % T.rank_of(R)
+    ids = [DstId(rid=topo.addr(c)[0], pnc=topo.addr(c)[1]) for c in cores]
+    return RemoteDMATransfer(dst_ids=ids, dma_engine_mask=bits_of(engines), remote_sem=T.sem[sem], srcs=[src], dsts=outs)
 
 
 def helper_program(g, core, R, T, topo):
-    dests, c1, c2, ha, hb = roads(R, T, topo)
-    if core not in (c1, c2, ha, hb):
-        return
-    out = topo.engines(core, dests[-1])
-    mask, ne = bits_of(out), len(out)
-    off, inner = engine_sets(R, core, dests[0], topo)
-    codes = core in (c1, ha)
-    mine = [0, 1, 2] if core in (c1, c2) else [3, 4]
-    g.wait_ge(T.sem.hpl, len(off) if codes else len(inner))
-    if codes:
-        src = T.hq[:, 0:NBIT].bitcast(dt.uint8)
-        ds = [T.pc[:, A0 + NBIT * j:A0 + NBIT * (j + 1)].bitcast(dt.uint8) for j in mine]
-    else:
-        src = T.hqz[:, 0:NBIT]
-        ds = [T.pz[:, A0 + NBIT * j:A0 + NBIT * (j + 1)] for j in mine]
-    g.remote_dma_fused([copy_to([dests[j] for j in mine], src, ds, mask, T.sem.pls, topo)], local_sem=T.sem.ls)
-    total = ne
-    if core in (ha, hb):
-        j = 3 if core == ha else 4
-        sem = T.sem["tb%d" % T.rank_of(R)]
-        rid, pid, _ = topo.addr(dests[j])
-        g.wait_ge(T.sem.hzs, len(inner))
-        g.remote_dma(T["tz%d" % j][:, 0:K], T.hz[:, 0:K], sem, T.sem.ls, pid, rid, mask)
-        g.wait_ge(T.sem.hcs, len(inner))
-        g.remote_dma(T["tc%d" % j][:, 0:K].bitcast(dt.uint8), T.hc[:, 0:K].bitcast(dt.uint8), sem, T.sem.ls, pid, rid, mask)
-        total += 2 * ne
-    g.wait_ge(T.sem.ls, total)
+    dests, helpers = roads(R, T, topo)
+    sets = engine_sets(R, T, topo)
+    for h, words in HANDED.items():
+        if helpers[h] != core:
+            continue
+        for word in words.split():
+            fed = [w[1] for call in CALLS for w in call.split() if w[0] == word[0] and h in w[2:]][0]
+            g.wait_ge(T.sem["f" + word[0]], len(sets[fed]))
+            g.remote_dma_fused([transfer(word[0], word[2:], sets[word[1]], R, T, topo)], local_sem=T.sem.ls)
+        g.wait_ge(T.sem.ls, sum(len(sets[w[1]]) for w in words.split()))
 
 
 def rank_program(g, core, T, topo):
@@ -122,198 +153,196 @@ def rank_program(g, core, T, topo):
             if topo.chip(R) == topo.chip(core):
                 helper_program(g, core, R, T, topo)
         return
-    dests, c1, c2, ha, hb = roads(core, T, topo)
     slot_q = [[T.rank_of(c) for c in T.cores if c != core and roads(c, T, topo)[0][j] == core][0] for j in range(N - 1)] + [rank]
-    off, inner = engine_sets(core, ha, dests[0], topo)
-
-    queue = {"v": g.vector, "s": g.scalar, "t": g.tensor, "y": g.sync, "g": g}
-    own_sem = {"v": "sv", "s": "ss", "t": "st"}
-    count = {"v": 0, "s": 0, "t": 0}
-    seen = {}
-
-    def need(q, sem, val):
-        if seen.get((q, sem), 0) < val:
-            seen[(q, sem)] = val
-            queue[q].wait_ge(T.sem[sem], val)
-
-    def done(q, ins):
-        ins.then_inc(T.sem[own_sem[q]], 1)
-        count[q] += 1
-        return (own_sem[q], count[q])
-
+    sets = engine_sets(core, T, topo)
+    V, S, PE, ALU = g.vector, g.scalar, g.tensor, AluOpType
     COPY = ActivationFunctionType.Copy
 
-    def move(q, out, in_, after):
-        for s, v in after:
-            need(q, s, v)
-        if q == "v":
-            return done("v", g.vector.tensor_copy(out, in_))
-        return done("s", g.scalar.activation(out, in_, COPY))
+    plan = {"v": [], "s": [], "t": [], "g": []}
+    own_sem = {"v": "sv", "s": "ss", "t": "st", "g": "sg"}
+    queue = {"v": V, "s": S, "t": PE, "g": g, "y": g.sync}
+    mark = {"hp": ("ldh", 16), "e": ("lde", 16), "own": ("own", 32)}
+    for word in LOADS.split():
+        mark[word] = ("ld" + word, 16)
+    far = [w for call in CALLS for w in call.split()] + [w for words in HANDED.values() for w in words.split()]
+    for st in STAGES:
+        mark["planes", st] = ("pl" + st, sum(len(sets[w[1]]) for w in far for j in STAGES[st][0] if w[0] in "pz" and str(j) in w))
+    for j in range(N - 1):
+        mark["table", j] = ("tb%d" % slot_q[j], sum(len(sets[w[1]]) for w in far if w[0] in "ABCS" and str(j) in w))
+    mark["table", OWN] = None
+    seen = {}
 
-    def quantise(out, scales, in_, after):
-        for s, v in after:
-            need("v", s, v)
-        return done("v", g.vector.quantize_mx(out, scales, in_))
+    def put(q, name, call, *after):
+        plan[q].append((call, after))
+        mark[name] = (own_sem[q], len(plan[q]))
 
-    g.sync.dma_start(T.hpt[:, 4 * ZL:4 * (ZL + NBIT)], T.hp[:, 0:4 * NBIT]).then_inc(T.sem.ldh, 16)
+    def need(q, *after):
+        for name in after:
+            sem, val = mark[name]
+            if seen.get((q, sem), 0) < val:
+                seen[q, sem] = val
+                queue[q].wait_ge(T.sem[sem], val)
+
+    def issue(q):
+        for call, after in plan[q]:
+            need(q, *after)
+            call().then_inc(T.sem[own_sem[q]], 1)
+
+    def move(q, name, out, in_, *after):
+        put(q, name, (lambda: V.tensor_copy(out, in_)) if q == "v" else (lambda: S.activation(out, in_, COPY)), *after)
+
+    def scalar_op(name, out, in_, a, b, op0, op1, *after):
+        put("v", name, lambda: V.tensor_scalar(out, in_, a, b, op0, op1), *after)
+
+    def fill(name, ap, value, *after):
+        put("v", name, lambda: V.memset(ap, value), *after)
+
+    def quantise(name, c, z, a, b, in_, *after):
+        put("v", name, lambda: V.quantize_mx(c[:, a:b], z[:, a:b], in_), *after)
+
+    reader = [None] * BANKS
+    bank_of = {}
+
+    def take(name, read_by):
+        b = len(bank_of) % BANKS
+        bank_of[name] = T["pb%d" % b]
+        last, reader[b] = reader[b], read_by
+        return bank_of[name], ([last] if last else [])
+
+    def product(slot, o):
+        c, z = table(T, slot)
+        pb, free = take(("m", slot, o), ("d", slot, o))
+        put("t", ("m", slot, o), lambda: PE.matmul_mx(pb[:, 0:K], T.wc[:, W * o:W * o + W], T.wz[:, W * o:W * o + W], c[:, 0:K], z[:, 0:K], True, True),
+            ("table", slot), ("qw", o), *free)
+
+    def signs(st, b):
+        slots, at, _, _, cuts = STAGES[st]
+        lo, hi = cuts[b], cuts[b + 1]
+        pb, free = take(("sg", st, b), ("bits", st, b))
+        for i in range(lo, hi):
+            a = at - NBIT * len(slots) * (i - lo)
+            put("t", ("sg", st, b), lambda i=i, a=a: PE.matmul_mx(
+                pb[:, 0:W], T.xc[:, GP * i:GP * i + W], T.xz[:, GP * i:GP * i + W], T.pc[:, a:a + W], T.pz[:, a:a + W],
+                i == lo, i == hi - 1), "q x", "q zeros", *(["own", ("planes", st)] if st != "o" else []), *free)
+
+    for word in TENSOR.split():
+        if word[0] == "g":
+            for b in [int(word[2])] if word[2:] else range(len(CUTS[word[1]][1]) - 1):
+                signs(word[1], b)
+        else:
+            for o in [int(word[2])] if word[2:] else (1, 0, 2):
+                product(int(word[1]), o)
+
+    put("g", "p", lambda: g.iota(T.part[:, 0:1], [[1, 1]], 0, 1))
+    put("g", "pf", lambda: g.iota(T.num[:, 0:1], [[1, 1]], 0, 1, allow_small_or_imprecise_dtypes=True))
+    put("g", "steps", lambda: g.iota(T.num[:, 4:4 + N], [[NBIT, N]], NBIT, 0, allow_small_or_imprecise_dtypes=True))
+
+    zeros = T.hpt[:, 4 * NBIT:4 * (NBIT + W)]
+    fill("zeros", zeros, 0.0)
+    fill("half", T.coef[:, :], 0.5)
+    put("v", "group", lambda: V.tensor_scalar(T.part[:, 1:2], T.part[:, 0:1], GP.bit_length() - 1, None, ALU.arith_shift_right), "p")
+    quantise("q zeros", T.pc, T.pz, 0, W, zeros, "zeros")
+    scalar_op("m - g", T.turn[:, 0:1], T.part[:, 1:2], -float(GP + 1), T.num[:, 0:1], ALU.mult, ALU.add, "group", "pf")
+    quantise("q zeros", T.pc, T.pz, ZEROS[1], ZEROS[1] + W, zeros)
+    scalar_op("wrap", T.turn[:, 1:2], T.turn[:, 0:1], 0.0, float(NC), ALU.is_lt, ALU.mult, "m - g")
+    quantise("q hp", T.pc, T.pz, W, 2 * W, T.hpt[:, 0:4 * W], "hp")
+    scalar_op("window", T.turn[:, 2:3], T.turn[:, 0:1], T.turn[:, 1:2], float(NC - 1), ALU.add, ALU.min, "wrap")
+    quantise("q zeros", T.pc, T.pz, ZEROS[2], ZEROS[2] + W, zeros)
+    put("v", "start", lambda: V.tensor_scalar(T.turn[:, 4:4 + N], T.num[:, 4:4 + N], T.turn[:, 2:3], None, ALU.mult), "window", "steps")
+    fill("coef", T.coef[:, 0:TOK:NBIT], 0.0, "half")
+    quantise(("table", OWN), T.ec, T.ez, 0, K, T.et[:, :], "e")
+    for st, (slots, _, _, col, _) in STAGES.items():
+        k = len(slots)
+        scalar_op(("off", st), T.off[:, col:col + k], T.num[:, 4:4 + k], T.turn[:, 3 + k:4 + k], -1.0, ALU.add, ALU.add, "start")
+
+    def behind(q, word):
+        kind, a = word[0], word[1:2]
+        if kind in "dp":
+            slot, o = int(a), int(word[2])
+            at = (slot * O + o) * K
+            if kind == "d":
+                move(q, ("d", slot, o), T.pr[:, at:at + K], bank_of["m", slot, o][:, 0:K], ("m", slot, o))
+            else:
+                y, l = (slot_q[slot] * O + o) * TOK, GP * PLACE.index(slot)
+                move(q, ("p", slot, o), T.yo[:, y:y + TOK], T.pr[:, at:at + K].indirect(T.li[:, l:l + NC]),
+                     ("d", slot, o), ("list", stage_of(slot)))
+        elif kind == "w":
+            lo, hi = int(a), int(word[2])
+            quantise("q qw", T.wc, T.wz, W * lo, W * hi, T.qwt[:, 4 * W * lo:4 * W * hi], word)
+            for o in range(lo, hi):
+                mark["qw", o] = mark["q qw"]
+        elif kind == "x":
+            quantise("q x", T.xc, T.xz, 0, TOK, T.xs[:, :], word)
+            quantise("q x", T.xc, T.xz, TOK, TOK + W, T.xs[:, 0:4 * W])
+        elif kind == "y":
+            fill("probe", T.probe[:, 0:100 * int(a)], 0.0)
+        elif kind == "k":
+            if a == "0":
+                move(q, "bk rows", T.bf[0:32, :], T.li[0:32, :], *[("list", st) for st in STAGES])
+            else:
+                put(q, "bk", lambda: V.transpose(T.bt[0:32, :], T.bf[0:32, :]), "bk rows")
+        else:
+            slots, _, at, col, cuts = STAGES[a]
+            k = len(slots)
+            step = NBIT * k
+            if kind == "b":
+                b = int(word[2])
+                lo, hi = at + step * cuts[b], at + step * cuts[b + 1]
+                scalar_op(("bits", a, b), T.bits[:, lo:hi], bank_of["sg", a, b][:, 0:hi - lo], 0.0, float(K // 2), ALU.is_gt, ALU.mult, ("sg", a, b))
+            elif kind == "s":
+                b0, b1 = int(word[2]), int(word[3])
+                lo, hi = at + step * cuts[b0], at + step * cuts[b1]
+                put(q, ("scan", a), lambda: V.tensor_tensor_scan(T.sc[:, lo:hi], T.coef[:, 0:hi - lo], T.bits[:, lo:hi], 0.0, ALU.mult, ALU.add),
+                    ("bits", a, b1 - 1), "coef")
+            else:
+                l = GP * PLACE.index(slots[0])
+                move(q, ("list", a), T.li[:, l:l + GP * k], T.sc[:, at:at + step * NC].indirect(T.off[:, col:col + k]),
+                     ("scan", a), ("off", a))
+
+    for q, order in (("v", VECTOR), ("s", SCALAR)):
+        for word in order.split():
+            behind(q, word)
+
+    g.sync.dma_start(T.hpt[:, 0:4 * NBIT], T.hp[:, 0:4 * NBIT]).then_inc(T.sem.ldh, 16)
     g.sync.dma_start(T.et[:, :], T.e[:, :]).then_inc(T.sem.lde, 16)
-    g.sync.dma_start(T.xs[:, :, :], T.x[:, :]).then_inc(T.sem.ldx, 16)
-    g.sync.dma_start(T.qwt[:, :], T.qw[:, :]).then_inc(T.sem.ldw, 16)
+    for word in LOADS.split():
+        if word == "x":
+            g.sync.dma_start(T.xs[:, :], T.x[:, :]).then_inc(T.sem.ldx, 16)
+        else:
+            lo, hi = 4 * W * int(word[1]), 4 * W * int(word[2])
+            g.sync.dma_start(T.qwt[:, lo:hi], T.qw[:, lo:hi]).then_inc(T.sem["ld" + word], 16)
+    need("y", "q hp")
+    for what in "pz":
+        g.sync.dma_start(planes(T, GAP, what), planes(T, W + NBIT, what)).then_inc(T.sem.own, 16)
 
-    z = done("v", g.vector.memset(T.hpt[:, 4 * (ZL + NBIT):4 * (ZL + 128)], 0.0))
-    half = done("v", g.vector.memset(T.coef[:, :], 0.5))
-    b0 = done("v", g.vector.memset(T.bf[:, :], 0.0))
-    done("v", g.vector.memset(T.hpt[:, 0:4 * ZL], 0.0))
-    zz = done("v", g.vector.memset(T.zt[:, :], 0.0))
-    qh = quantise(T.hq[:, :], T.hqz[:, :], T.hpt[:, 4 * ZL:4 * (ZL + 128)], [("ldh", 16), z])
-    quantise(T.pc[:, 0:A0], T.pz[:, 0:A0], T.zt[:, :], [zz])
-    quantise(T.pc[:, Z1:Z1 + 128], T.pz[:, Z1:Z1 + 128], T.zt[:, :], [])
-    quantise(T.oc[:, :], T.oz[:, :], T.hpt[:, :], [])
-    half = done("v", g.vector.memset(T.coef[:, 0:3 * NR:NBIT], 0.0))
-    qe = quantise(T.ec[:, :], T.ez[:, :], T.et[:, :], [("lde", 16)])
-    cp = []
-    for k in range(8):
-        cp.append(move("s" if k < 3 else "v", T.xrep[:, :, 64 * k:64 * k + 64], T.xs[:, :, :], [("ldx", 16)]))
-    qw = quantise(T.wc[:, :], T.wz[:, :], T.qwt[:, :], [("ldw", 16)])
-    qx = [quantise(T.xc[:, 128 * i:128 * i + 128], T.xz[:, 128 * i:128 * i + 128], T.xrep[:, i, :], [cp[2], cp[7]]) for i in range(NC)]
-    need("y", *qh)
-    g.sync.dma_start(T.pc[:, GAP:Z1].bitcast(dt.uint8), T.hq[:, NBIT:2 * NBIT].bitcast(dt.uint8)).then_inc(T.sem.gap, 16)
-    g.sync.dma_start(T.pz[:, GAP:Z1], T.hqz[:, NBIT:2 * NBIT]).then_inc(T.sem.gap, 16)
+    for q in plan:
+        issue(q)
 
-    need("g", *qh)
-    pl = T.hq[:, 0:NBIT].bitcast(dt.uint8)
-    g.remote_dma_fused([copy_to([c1, ha], pl, [pl, pl], bits_of(off), T.sem.hpl, topo)], local_sem=T.sem.ls)
-    pl = T.hqz[:, 0:NBIT]
-    g.remote_dma_fused([copy_to([c2, hb], pl, [pl, pl], bits_of(inner), T.sem.hpl, topo)], local_sem=T.sem.ls)
-    need("g", *qe)
-    total = len(off) + len(inner)
-    for src, far, near, sem, codes in ((T.ez[:, 0:K], "tz", T.hz[:, 0:K], T.sem.hzs, False), (T.ec[:, 0:K], "tc", T.hc[:, 0:K], T.sem.hcs, True)):
-        fars = [T["%s%d" % (far, j)][:, 0:K] for j in range(3)]
-        if codes:
-            src, near, fars = src.bitcast(dt.uint8), near.bitcast(dt.uint8), [d.bitcast(dt.uint8) for d in fars]
-        g.remote_dma_fused([copy_to(dests[:3], src, fars, bits_of(off), T.sem["tb%d" % rank], topo),
-                            copy_to([ha, hb], src, [near, near], bits_of(inner), sem, topo)], local_sem=T.sem.ls)
-        total += len(off) + len(inner)
-
-    free = [None] * BANKS
-    unit = [0]
-
-    def bank():
-        b = unit[0] % BANKS
-        unit[0] += 1
-        if free[b] is not None:
-            need("t", *free[b])
-        return b
-
-    def products(cd, sc_, after):
-        res = []
-        for s, v in after:
-            need("t", s, v)
-        for o in range(O):
-            b = bank()
-            m = done("t", g.tensor.matmul_mx(T["pb%d" % b][:, 0:K], T.wc[:, 128 * o:128 * o + 128], T.wz[:, 128 * o:128 * o + 128],
-                                             cd[:, 0:K], sc_[:, 0:K], True, True))
-            res.append((b, m))
-        return res
-
-    def drain(q, slot, o, bm):
-        b, m = bm
-        a = (slot * O + o) * K
-        free[b] = move(q, T.pr[:, a:a + K], T["pb%d" % b][:, 0:K], [m])
-        return free[b]
-
-    def pick(q, slot, o, after):
-        r = slot_q[slot]
-        a, y = (slot * O + o) * K, (r * O + o) * TOK
-        return move(q, T.yo[:, y:y + TOK], T.pr[:, a:a + K].indirect(T.li[:, NC * r:NC * r + NC]), after)
+    sent = 0
+    for call in CALLS:
+        words = call.split()
+        need("g", "q hp" if words[0][0] in "pz" else ("table", OWN))
+        g.remote_dma_fused([transfer(w[0], w[2:], sets[w[1]], core, T, topo) for w in words], local_sem=T.sem.ls)
+        sent += sum(len(sets[w[1]]) for w in words)
 
     nst = [0]
 
-    def keep(out, in_, after):
-        for s, v in after:
-            need("y", s, v)
+    def keep(out, in_, *after):
+        need("y", *after)
         g.sync.dma_start(out, in_).then_inc(T.sem.yst, 16)
         nst[0] += 1
 
-    def store(slot, o0, o1, after):
-        y = (slot_q[slot] * O) * TOK
-        keep(T.y[:, y + o0 * TOK:y + o1 * TOK], T.yo[:, y + o0 * TOK:y + o1 * TOK], after)
-
-    def bucket_products(lo, hi, cd, sc_, at, step):
-        b = bank()
-        for i in range(lo, hi):
-            a = at - step * (i - lo)
-            m = done("t", g.tensor.matmul_mx(T["pb%d" % b][:, 0:128], T.xc[:, 128 * i:128 * i + 128], T.xz[:, 128 * i:128 * i + 128],
-                                             cd[:, a:a + 128], sc_[:, a:a + 128], i == lo, i == hi - 1))
-        return b, m
-
-    def numbers(bm, bits, out, n):
-        b, m = bm
-        need("v", *m)
-        free[b] = done("v", g.vector.tensor_scalar(bits, T["pb%d" % b][:, 0:n], 0.0, 128.0, AluOpType.is_gt, AluOpType.mult))
-        need("v", *free[b])
-        need("v", *half)
-        return done("v", g.vector.tensor_tensor_scan(out, T.coef[:, 0:n], bits, 0.0, AluOpType.mult, AluOpType.add))
-
-    own = N - 1
-    bm = products(T.ec, T.ez, [qe, qw])
-    dr = [drain("s", own, o, bm[o]) for o in range(O)]
-    need("t", *qx[-1])
-    s = numbers(bucket_products(0, NC, T.oc, T.oz, ZL, NBIT), T.obits[:, :], T.osc[:, :], NC * NBIT)
-    li = {own: move("v", T.li[:, NC * rank:NC * rank + NC], T.osc[:, NBIT - 1:NC * NBIT:NBIT], [s])}
-    store(own, 0, O, [pick("s", own, o, [dr[o], li[own]]) for o in range(O)])
-
-    need("t", "gap", 32)
-    need("t", "pls", 2 * len(off) * (N - 1))
-    groups = [bucket_products(lo, hi, T.pc, T.pz, A0, NR) for lo, hi in GROUPS]
-    scans = [numbers(groups[k], T.bits[:, NR * lo:NR * hi], T.sc[:, NR * lo:NR * hi], NR * (hi - lo)) for k, (lo, hi) in enumerate(GROUPS)]
-
-    def make_list(slot):
-        r = slot_q[slot]
-        li[slot] = move("v", T.li[:, NC * r:NC * r + NC], T.sc[:, NBIT * slot + NBIT - 1:NC * NR:NR], [scans[-1]])
-
-    pm, dr = {}, {}
-
-    def fetch(slot):
-        pm[slot] = products(T["tc%d" % slot], T["tz%d" % slot], [("tb%d" % slot_q[slot], 2 * len(off))])
-
-    make_list(0)
-    make_list(1)
-    fetch(0)
-    for o in range(O):
-        dr[0, o] = drain("s", 0, o, pm[0][o])
-    last = N - 2
-    for slot in range(N - 1):
-        nxt = slot + 1
-        if nxt <= last:
-            fetch(nxt)
-        p0 = pick("v", slot, 0, [dr[slot, 0], li[slot]])
-        if nxt <= last:
-            dr[nxt, 0] = drain("v", nxt, 0, pm[nxt][0])
-        p1 = pick("s", slot, 1, [dr[slot, 1], li[slot]])
-        if nxt <= last:
-            dr[nxt, 1] = drain("s", nxt, 1, pm[nxt][1])
-        p2 = pick("v", slot, 2, [dr[slot, 2]])
-        if nxt <= last:
-            dr[nxt, 2] = drain("s", nxt, 2, pm[nxt][2])
-        if slot < last:
-            if nxt < last:
-                make_list(nxt + 1)
-            store(slot, 0, O, [p0, p1, p2])
+    for word in STORES.split():
+        if word == "k":
+            for i, slot in enumerate(PLACE):
+                p, c = GP * (i % 2), 2 * GP * (i // 2)
+                keep(T.bk[slot_q[slot], :], T.bt[p:p + NC, c:c + GP], "bk")
         else:
-            store(slot, 0, 2, [p0, p1])
-            store(slot, 2, O, [p2])
+            slot, o0, o1 = (int(ch) for ch in word)
+            y = slot_q[slot] * O * TOK
+            keep(T.y[:, y + o0 * TOK:y + o1 * TOK], T.yo[:, y + o0 * TOK:y + o1 * TOK], *[("p", slot, o) for o in range(o0, o1)])
 
-    need("v", *b0)
-    h = NC * N // 2
-    move("v", T.bf[0:32, 0:h], T.li[0:32, 0:h], [li[N - 2]])
-    f = move("v", T.bf[0:32, 32:32 + h], T.li[0:32, h:2 * h], [])
-    need("v", *f)
-    tr = done("v", g.vector.transpose(T.bt[0:32, :], T.bf[0:32, :]))
-    keep(T.bk[0:N // 2, :], T.bt[0:h, 0:16], [tr])
-    keep(T.bk[N // 2:N, :], T.bt[0:h, 32:48], [])
-
-    need("y", "yst", 16 * nst[0])
-    need("g", "ls", total)
-    for q in ("v", "s", "t"):
-        need("g", own_sem[q], count[q])
+    g.sync.wait_ge(T.sem.yst, 16 * nst[0])
+    g.wait_ge(T.sem.ls, sent)
+    for q in plan:
+        g.wait_ge(T.sem[own_sem[q]], len(plan[q]))

@@ -5,21 +5,21 @@ N, TOK, NBIT, K, O = 6, 160, 8, 256, 3
 GP = 16
 NC = TOK // GP
 W = 128
-CUT = (0, 5 * K // 8, K)
+CUT = (0, 9 * K // 16, K)
 BANKS = 8
 OWN = N - 1
 
-CALLS = ("po01 pia", "zo01 zib", "So0 Sic", "Ao0 Aia", "Bo0 Bib")
-HANDED = {"a": "po234 Ao1234", "b": "zo234 Bo1234", "c": "So1234"}
+CALLS = ("po01 pia", "zo01 zib", "So0 Sic", "Bib", "Co0", "Aia", "zo2")
+HANDED = {"a": "po234 Ao1234", "b": "zo34 Bo1234", "c": "So2134"}
 
 CUTS = {"o": ([OWN], (0, NC)), "a": ([0, 1], (0, 8, NC)), "b": ([2, 3, 4], (0, 5, NC))}
 
 LOADS = "x w03"
-TENSOR = "go m5 ga m0 gb0 m1 gb1 m2 m3 m4"
-VECTOR = ("x w03 bo0 so01 lo d52 p50 p52 ba0 sa01 ba1 sa12 la bb0 sb01 d12 bb1 p12 sb12 p10 lb d22 k0 p22 k1 d32 p20 p32 "
+TENSOR = "go m5 ga m0 gb0 m1 gb1 m2210 m3210 m4210"
+VECTOR = ("x w03 bo0 so01 lo d52 ba0 ba1 sa02 la k00 k10 d02 bb0 p02 sb01 d12 bb1 p12 sb12 d22 lb d32 p22 k01 p20 k11 p32 "
           "d42 p30 p42 p40")
-SCALAR = "d51 d50 p51 d01 d00 d02 p01 p00 p02 d11 d10 p11 d21 d20 p21 d31 d30 p31 d41 d40 p41"
-STORES = "503 003 103 k 203 303 413 401"
+SCALAR = "d51 d50 p51 p50 p52 d01 d00 p01 p00 d11 d10 p11 p10 d21 d20 p21 d31 d30 p31 d41 d40 p41"
+STORES = "503 k0 003 103 203 313 k1 301 s413 401"
 
 
 def lay_out():
@@ -54,7 +54,7 @@ SCRATCH = {
     "xz": ("sbuf", [128, TOK + W], "uint8"),
     "wc": ("sbuf", [128, O * W], "float8_e4m3fn_x4"),
     "wz": ("sbuf", [128, O * W], "uint8"),
-    "probe": ("sbuf", [128, 1024], "float32"),
+    "probe": ("sbuf", [128, 2048], "float32"),
     "part": ("sbuf", [128, 2], "int32"),
     "num": ("sbuf", [128, 16], "float32"),
     "turn": ("sbuf", [128, 16], "float32"),
@@ -63,8 +63,8 @@ SCRATCH = {
     "bits": ("sbuf", [128, N * NBIT * NC], "bfloat16"),
     "sc": ("sbuf", [128, N * NBIT * NC], "bfloat16"),
     "li": ("sbuf", [128, GP * N], "uint16"),
-    "bf": ("sbuf", [128, GP * N], "float32"),
-    "bt": ("sbuf", [128, GP * N], "float32"),
+    "bf": ("sbuf", [128, 128], "float32"),
+    "bt": ("sbuf", [128, 128], "float32"),
     "pr": ("sbuf", [128, N * O * K], "float32"),
     "yo": ("sbuf", [128, N * O * TOK], "float32"),
 }
@@ -90,7 +90,7 @@ def roads(R, T, topo):
     diag = [c for c in far if c not in plane and c not in mate]
     near = sorted((c for c in topo.cores_of(R) if c != R), key=lambda c: topo.die(c) != topo.die(R))
     owners = [c for c in near if all(topo.may_write(c, d) for d in far)]
-    return mate + plane + diag, dict(zip("abcdefg", owners + [c for c in near if c not in owners]))
+    return plane[:1] + mate + plane[1:] + diag, dict(zip("abcdefg", owners + [c for c in near if c not in owners]))
 
 
 def engine_sets(R, T, topo):
@@ -166,15 +166,19 @@ def rank_program(g, core, T, topo):
         mark[word] = ("ld" + word, 16)
     far = [w for call in CALLS for w in call.split()] + [w for words in HANDED.values() for w in words.split()]
     for st in STAGES:
-        mark["planes", st] = ("pl" + st, sum(len(sets[w[1]]) for w in far for j in STAGES[st][0] if w[0] in "pz" and str(j) in w))
+        mark["planes", st] = ("pl" + st, sum(len(sets[w[1]]) * len(w[2:]) for w in far for j in STAGES[st][0] if w[0] in "pz" and str(j) == w[2]))
     for j in range(N - 1):
         mark["table", j] = ("tb%d" % slot_q[j], sum(len(sets[w[1]]) for w in far if w[0] in "ABCS" and str(j) in w))
     mark["table", OWN] = None
     seen = {}
 
+    count = dict.fromkeys(plan, 0)
+
     def put(q, name, call, *after):
-        plan[q].append((call, after))
-        mark[name] = (own_sem[q], len(plan[q]))
+        plan[q].append((name, call, after))
+        if name is not None:
+            count[q] += 1
+            mark[name] = (own_sem[q], count[q])
 
     def need(q, *after):
         for name in after:
@@ -184,9 +188,11 @@ def rank_program(g, core, T, topo):
                 queue[q].wait_ge(T.sem[sem], val)
 
     def issue(q):
-        for call, after in plan[q]:
+        for name, call, after in plan[q]:
             need(q, *after)
-            call().then_inc(T.sem[own_sem[q]], 1)
+            done = call()
+            if name is not None:
+                done.then_inc(T.sem[own_sem[q]], 1)
 
     def move(q, name, out, in_, *after):
         put(q, name, (lambda: V.tensor_copy(out, in_)) if q == "v" else (lambda: S.activation(out, in_, COPY)), *after)
@@ -221,16 +227,16 @@ def rank_program(g, core, T, topo):
         pb, free = take(("sg", st, b), ("bits", st, b))
         for i in range(lo, hi):
             a = at - NBIT * len(slots) * (i - lo)
-            put("t", ("sg", st, b), lambda i=i, a=a: PE.matmul_mx(
+            put("t", ("sg", st, b) if i == hi - 1 else None, lambda i=i, a=a: PE.matmul_mx(
                 pb[:, 0:W], T.xc[:, GP * i:GP * i + W], T.xz[:, GP * i:GP * i + W], T.pc[:, a:a + W], T.pz[:, a:a + W],
-                i == lo, i == hi - 1), "q x", "q zeros", *(["own", ("planes", st)] if st != "o" else []), *free)
+                i == lo, i == hi - 1), "q x", "q zeros", *({"o": [], "a": [("planes", st)], "b": ["own", ("planes", "a"), ("planes", st)]}[st]), *free)
 
     for word in TENSOR.split():
         if word[0] == "g":
             for b in [int(word[2])] if word[2:] else range(len(CUTS[word[1]][1]) - 1):
                 signs(word[1], b)
         else:
-            for o in [int(word[2])] if word[2:] else (1, 0, 2):
+            for o in [int(ch) for ch in word[2:]] if word[2:] else (1, 0, 2):
                 product(int(word[1]), o)
 
     put("g", "p", lambda: g.iota(T.part[:, 0:1], [[1, 1]], 0, 1))
@@ -239,7 +245,9 @@ def rank_program(g, core, T, topo):
 
     zeros = T.hpt[:, 4 * NBIT:4 * (NBIT + W)]
     fill("zeros", zeros, 0.0)
-    fill("half", T.coef[:, :], 0.5)
+    put("s", "half", lambda: S.activation(T.coef[:, :], zeros[:, 0:TOK], ActivationFunctionType.Identity, bias=0.5), "zeros")
+    move("s", "pad", T.bf[0:32, :], zeros[0:32, 0:W])
+    move("s", "coef", T.coef[:, ::NBIT], zeros[:, 0:TOK // NBIT], "half")
     put("v", "group", lambda: V.tensor_scalar(T.part[:, 1:2], T.part[:, 0:1], GP.bit_length() - 1, None, ALU.arith_shift_right), "p")
     quantise("q zeros", T.pc, T.pz, 0, W, zeros, "zeros")
     scalar_op("m - g", T.turn[:, 0:1], T.part[:, 1:2], -float(GP + 1), T.num[:, 0:1], ALU.mult, ALU.add, "group", "pf")
@@ -249,7 +257,6 @@ def rank_program(g, core, T, topo):
     scalar_op("window", T.turn[:, 2:3], T.turn[:, 0:1], T.turn[:, 1:2], float(NC - 1), ALU.add, ALU.min, "wrap")
     quantise("q zeros", T.pc, T.pz, ZEROS[2], ZEROS[2] + W, zeros)
     put("v", "start", lambda: V.tensor_scalar(T.turn[:, 4:4 + N], T.num[:, 4:4 + N], T.turn[:, 2:3], None, ALU.mult), "window", "steps")
-    fill("coef", T.coef[:, 0:TOK:NBIT], 0.0, "half")
     quantise(("table", OWN), T.ec, T.ez, 0, K, T.et[:, :], "e")
     for st, (slots, _, _, col, _) in STAGES.items():
         k = len(slots)
@@ -275,12 +282,16 @@ def rank_program(g, core, T, topo):
             quantise("q x", T.xc, T.xz, 0, TOK, T.xs[:, :], word)
             quantise("q x", T.xc, T.xz, TOK, TOK + W, T.xs[:, 0:4 * W])
         elif kind == "y":
-            fill("probe", T.probe[:, 0:100 * int(a)], 0.0)
+            move(q, "probe", T.probe[:, 0:O * K], T.pr[:, OWN * O * K:N * O * K], *[("d", OWN, o) for o in range(O)])
+        elif kind == "z":
+            move(q, "probe2", T.probe[:, O * K:2 * O * K], T.pr[:, OWN * O * K:N * O * K], *[("d", OWN, o) for o in range(O)])
         elif kind == "k":
+            h, n = int(word[2]), GP * N // 2
             if a == "0":
-                move(q, "bk rows", T.bf[0:32, :], T.li[0:32, :], *[("list", st) for st in STAGES])
+                move(q, ("bk rows", h), T.bf[0:32, 64 * h:64 * h + n], T.li[0:32, n * h:n * h + n], "pad",
+                     *[("list", stage_of(slot)) for slot in PLACE[N // 2 * h:N // 2 * (h + 1)]])
             else:
-                put(q, "bk", lambda: V.transpose(T.bt[0:32, :], T.bf[0:32, :]), "bk rows")
+                put(q, ("bk", h), lambda: V.transpose(T.bt[0:32, 64 * h:64 * h + 64], T.bf[0:32, 64 * h:64 * h + 64]), ("bk rows", h))
         else:
             slots, _, at, col, cuts = STAGES[a]
             k = len(slots)
@@ -327,22 +338,24 @@ def rank_program(g, core, T, topo):
 
     nst = [0]
 
-    def keep(out, in_, *after):
-        need("y", *after)
-        g.sync.dma_start(out, in_).then_inc(T.sem.yst, 16)
+    def keep(out, in_, *after, q="y"):
+        need(q, *after)
+        queue[q].dma_start(out, in_).then_inc(T.sem.yst, 16)
         nst[0] += 1
 
     for word in STORES.split():
-        if word == "k":
-            for i, slot in enumerate(PLACE):
-                p, c = GP * (i % 2), 2 * GP * (i // 2)
-                keep(T.bk[slot_q[slot], :], T.bt[p:p + NC, c:c + GP], "bk")
+        if word[0] == "k":
+            h = int(word[1])
+            for i, slot in enumerate(PLACE[N // 2 * h:N // 2 * (h + 1)]):
+                p, c = GP * (i % 2), 64 * h + 2 * GP * (i // 2)
+                keep(T.bk[slot_q[slot], :], T.bt[p:p + NC, c:c + GP], ("bk", h))
         else:
-            slot, o0, o1 = (int(ch) for ch in word)
+            slot, o0, o1 = (int(ch) for ch in word[-3:])
             y = slot_q[slot] * O * TOK
-            keep(T.y[:, y + o0 * TOK:y + o1 * TOK], T.yo[:, y + o0 * TOK:y + o1 * TOK], *[("p", slot, o) for o in range(o0, o1)])
+            keep(T.y[:, y + o0 * TOK:y + o1 * TOK], T.yo[:, y + o0 * TOK:y + o1 * TOK], *[("p", slot, o) for o in range(o0, o1)],
+                 q=word[:-3] or "y")
 
     g.sync.wait_ge(T.sem.yst, 16 * nst[0])
     g.wait_ge(T.sem.ls, sent)
     for q in plan:
-        g.wait_ge(T.sem[own_sem[q]], len(plan[q]))
+        g.wait_ge(T.sem[own_sem[q]], count[q])

from concourse.bass import DstId, RemoteDMATransfer
from concourse.mybir import dt, AluOpType, ActivationFunctionType

N, TOK, NBIT, K, O = 6, 160, 8, 256, 3
GP = 16
NC = TOK // GP
W = 128
CUT = (0, 9 * K // 16, K)
BANKS = 8
OWN = N - 1

CALLS = ("po01 pia", "zo01 zib", "So0 Sic", "Bib", "Co0", "Aia", "zo2")
HANDED = {"a": "po234 Ao1234", "b": "zo34 Bo1234", "c": "So2134"}

CUTS = {"o": ([OWN], (0, NC)), "a": ([0, 1], (0, 8, NC)), "b": ([2, 3, 4], (0, 5, NC))}

LOADS = "x w03"
TENSOR = "go m5 ga m0 gb0 m1 gb1 m2210 m3210 m4210"
VECTOR = ("x w03 bo0 so01 lo d52 ba0 ba1 sa02 la k00 k10 d02 bb0 p02 sb01 d12 bb1 p12 sb12 d22 lb d32 p22 k01 p20 k11 p32 "
          "d42 p30 p42 p40")
SCALAR = "d51 d50 p51 p50 p52 d01 d00 p01 p00 d11 d10 p11 p10 d21 d20 p21 d31 d30 p31 d41 d40 p41"
STORES = "503 k0 003 103 203 313 k1 301 s413 401"


def lay_out():
    stages, at, sc, off, zeros, gap = {}, W, 0, 0, [0], None
    for st, (slots, cuts) in CUTS.items():
        stages[st] = (slots, at, sc, off, cuts)
        sc, off = sc + NBIT * len(slots) * NC, off + len(slots) + len(slots) % 2
        if st == "o":
            at += W
            continue
        at += NBIT * len(slots)
        if len(slots) % 2:
            gap, at = at, at + NBIT
        zeros.append(at)
        at += W
    return stages, at, zeros, gap


STAGES, PC, ZEROS, GAP = lay_out()
PLACE = [slot for slots, _ in CUTS.values() for slot in slots]

SCRATCH = {
    "hpt": ("sbuf", [128, 4 * (NBIT + W)], "bfloat16"),
    "et": ("sbuf", [128, 4 * K], "bfloat16"),
    "xs": ("sbuf", [128, 4 * TOK], "bfloat16"),
    "qwt": ("sbuf", [128, O * 512], "bfloat16"),
    "pc": ("sbuf", [128, PC], "float8_e4m3fn_x4"),
    "pz": ("sbuf", [128, PC], "uint8"),
    "ec": ("sbuf", [128, K], "float8_e4m3fn_x4"),
    "ez": ("sbuf", [128, K], "uint8"),
    "xc": ("sbuf", [128, TOK + W], "float8_e4m3fn_x4"),
    "xz": ("sbuf", [128, TOK + W], "uint8"),
    "wc": ("sbuf", [128, O * W], "float8_e4m3fn_x4"),
    "wz": ("sbuf", [128, O * W], "uint8"),
    "probe": ("sbuf", [128, 2048], "float32"),
    "part": ("sbuf", [128, 2], "int32"),
    "num": ("sbuf", [128, 16], "float32"),
    "turn": ("sbuf", [128, 16], "float32"),
    "off": ("sbuf", [128, 8], "uint16"),
    "coef": ("sbuf", [128, TOK], "bfloat16"),
    "bits": ("sbuf", [128, N * NBIT * NC], "bfloat16"),
    "sc": ("sbuf", [128, N * NBIT * NC], "bfloat16"),
    "li": ("sbuf", [128, GP * N], "uint16"),
    "bf": ("sbuf", [128, 128], "float32"),
    "bt": ("sbuf", [128, 128], "float32"),
    "pr": ("sbuf", [128, N * O * K], "float32"),
    "yo": ("sbuf", [128, N * O * TOK], "float32"),
}
for _j in range(N - 1):
    SCRATCH["tc%d" % _j] = ("sbuf", [128, K], "float8_e4m3fn_x4")
    SCRATCH["tz%d" % _j] = ("sbuf", [128, K], "uint8")
for _j in range(BANKS):
    SCRATCH["pb%d" % _j] = ("psum", [128, 512], "float32")

SEMAPHORES = (["lde", "ldh", "own", "sv", "ss", "st", "sg", "ls", "yst"] + ["f" + w for w in "pzABCS"] + ["ld" + w for w in LOADS.split()]
              + ["pl" + st for st in CUTS] + ["tb%d" % j for j in range(N)])


def bits_of(engines):
    return sum(1 << e for e in engines)


def roads(R, T, topo):
    me = T.rank_of(R)
    far = sorted((c for c in T.cores if c != R), key=lambda c: (T.rank_of(c) - me) % N)
    plane = [c for c in far if topo.same_plane(topo.chip(R), topo.chip(c))]
    mate = [c for c in far if topo.mates(topo.chip(R), topo.chip(c))]
    diag = [c for c in far if c not in plane and c not in mate]
    near = sorted((c for c in topo.cores_of(R) if c != R), key=lambda c: topo.die(c) != topo.die(R))
    owners = [c for c in near if all(topo.may_write(c, d) for d in far)]
    return plane[:1] + mate + plane[1:] + diag, dict(zip("abcdefg", owners + [c for c in near if c not in owners]))


def engine_sets(R, T, topo):
    dests, helpers = roads(R, T, topo)
    off, every = topo.engines(R, dests[0]), topo.engines(R, helpers["a"])
    inner, h = [e for e in every if e not in off], len(off) // 2
    return {"o": off, "i": inner, "a": every, "l": off[:h], "h": off[h:], "m": inner[:h], "n": inner[h:]}


def table(T, slot):
    return (T.ec, T.ez) if slot == OWN else (T["tc%d" % slot], T["tz%d" % slot])


def planes(T, at, what):
    return T.pc[:, at:at + NBIT].bitcast(dt.uint8) if what == "p" else T.pz[:, at:at + NBIT]


def stage_of(slot):
    return [st for st in STAGES if slot in STAGES[st][0]][0]


def piece(T, slot, what):
    if what in "pz":
        slots, at = STAGES[stage_of(OWN if slot is None else slot)][:2]
        return planes(T, at + NBIT * slots.index(OWN if slot is None else slot), what)
    c, z = table(T, OWN if slot is None else slot)
    lo, hi = {"A": CUT[:2], "B": CUT[1:], "C": (0, K), "S": (0, K)}[what]
    return z[:, lo:hi] if what == "S" else c[:, lo:hi].bitcast(dt.uint8)


def transfer(what, to, engines, R, T, topo):
    dests, helpers = roads(R, T, topo)
    src = piece(T, None, what)
    if to[0] in helpers:
        cores, outs, sem = [helpers[h] for h in to], [src] * len(to), "f" + what
    else:
        cores, outs = [dests[int(j)] for j in to], [piece(T, int(j), what) for j in to]
        sem = "pl" + stage_of(int(to[0])) if what in "pz" else "tb%d" % T.rank_of(R)
    ids = [DstId(rid=topo.addr(c)[0], pnc=topo.addr(c)[1]) for c in cores]
    return RemoteDMATransfer(dst_ids=ids, dma_engine_mask=bits_of(engines), remote_sem=T.sem[sem], srcs=[src], dsts=outs)


def helper_program(g, core, R, T, topo):
    dests, helpers = roads(R, T, topo)
    sets = engine_sets(R, T, topo)
    for h, words in HANDED.items():
        if helpers[h] != core:
            continue
        for word in words.split():
            fed = [w[1] for call in CALLS for w in call.split() if w[0] == word[0] and h in w[2:]][0]
            g.wait_ge(T.sem["f" + word[0]], len(sets[fed]))
            g.remote_dma_fused([transfer(word[0], word[2:], sets[word[1]], R, T, topo)], local_sem=T.sem.ls)
        g.wait_ge(T.sem.ls, sum(len(sets[w[1]]) for w in words.split()))


def rank_program(g, core, T, topo):
    rank = T.rank_of(core)
    if rank is None:
        for R in T.cores:
            if topo.chip(R) == topo.chip(core):
                helper_program(g, core, R, T, topo)
        return
    slot_q = [[T.rank_of(c) for c in T.cores if c != core and roads(c, T, topo)[0][j] == core][0] for j in range(N - 1)] + [rank]
    sets = engine_sets(core, T, topo)
    V, S, PE, ALU = g.vector, g.scalar, g.tensor, AluOpType
    COPY = ActivationFunctionType.Copy

    plan = {"v": [], "s": [], "t": [], "g": []}
    own_sem = {"v": "sv", "s": "ss", "t": "st", "g": "sg"}
    queue = {"v": V, "s": S, "t": PE, "g": g, "y": g.sync}
    mark = {"hp": ("ldh", 16), "e": ("lde", 16), "own": ("own", 32)}
    for word in LOADS.split():
        mark[word] = ("ld" + word, 16)
    far = [w for call in CALLS for w in call.split()] + [w for words in HANDED.values() for w in words.split()]
    for st in STAGES:
        mark["planes", st] = ("pl" + st, sum(len(sets[w[1]]) * len(w[2:]) for w in far for j in STAGES[st][0] if w[0] in "pz" and str(j) == w[2]))
    for j in range(N - 1):
        mark["table", j] = ("tb%d" % slot_q[j], sum(len(sets[w[1]]) for w in far if w[0] in "ABCS" and str(j) in w))
    mark["table", OWN] = None
    seen = {}

    count = dict.fromkeys(plan, 0)

    def put(q, name, call, *after):
        plan[q].append((name, call, after))
        if name is not None:
            count[q] += 1
            mark[name] = (own_sem[q], count[q])

    def need(q, *after):
        for name in after:
            sem, val = mark[name]
            if seen.get((q, sem), 0) < val:
                seen[q, sem] = val
                queue[q].wait_ge(T.sem[sem], val)

    def issue(q):
        for name, call, after in plan[q]:
            need(q, *after)
            done = call()
            if name is not None:
                done.then_inc(T.sem[own_sem[q]], 1)

    def move(q, name, out, in_, *after):
        put(q, name, (lambda: V.tensor_copy(out, in_)) if q == "v" else (lambda: S.activation(out, in_, COPY)), *after)

    def scalar_op(name, out, in_, a, b, op0, op1, *after):
        put("v", name, lambda: V.tensor_scalar(out, in_, a, b, op0, op1), *after)

    def fill(name, ap, value, *after):
        put("v", name, lambda: V.memset(ap, value), *after)

    def quantise(name, c, z, a, b, in_, *after):
        put("v", name, lambda: V.quantize_mx(c[:, a:b], z[:, a:b], in_), *after)

    reader = [None] * BANKS
    bank_of = {}

    def take(name, read_by):
        b = len(bank_of) % BANKS
        bank_of[name] = T["pb%d" % b]
        last, reader[b] = reader[b], read_by
        return bank_of[name], ([last] if last else [])

    def product(slot, o):
        c, z = table(T, slot)
        pb, free = take(("m", slot, o), ("d", slot, o))
        put("t", ("m", slot, o), lambda: PE.matmul_mx(pb[:, 0:K], T.wc[:, W * o:W * o + W], T.wz[:, W * o:W * o + W], c[:, 0:K], z[:, 0:K], True, True),
            ("table", slot), ("qw", o), *free)

    def signs(st, b):
        slots, at, _, _, cuts = STAGES[st]
        lo, hi = cuts[b], cuts[b + 1]
        pb, free = take(("sg", st, b), ("bits", st, b))
        for i in range(lo, hi):
            a = at - NBIT * len(slots) * (i - lo)
            put("t", ("sg", st, b) if i == hi - 1 else None, lambda i=i, a=a: PE.matmul_mx(
                pb[:, 0:W], T.xc[:, GP * i:GP * i + W], T.xz[:, GP * i:GP * i + W], T.pc[:, a:a + W], T.pz[:, a:a + W],
                i == lo, i == hi - 1), "q x", "q zeros", *({"o": [], "a": [("planes", st)], "b": ["own", ("planes", "a"), ("planes", st)]}[st]), *free)

    for word in TENSOR.split():
        if word[0] == "g":
            for b in [int(word[2])] if word[2:] else range(len(CUTS[word[1]][1]) - 1):
                signs(word[1], b)
        else:
            for o in [int(ch) for ch in word[2:]] if word[2:] else (1, 0, 2):
                product(int(word[1]), o)

    put("g", "p", lambda: g.iota(T.part[:, 0:1], [[1, 1]], 0, 1))
    put("g", "pf", lambda: g.iota(T.num[:, 0:1], [[1, 1]], 0, 1, allow_small_or_imprecise_dtypes=True))
    put("g", "steps", lambda: g.iota(T.num[:, 4:4 + N], [[NBIT, N]], NBIT, 0, allow_small_or_imprecise_dtypes=True))

    zeros = T.hpt[:, 4 * NBIT:4 * (NBIT + W)]
    fill("zeros", zeros, 0.0)
    put("s", "half", lambda: S.activation(T.coef[:, :], zeros[:, 0:TOK], ActivationFunctionType.Identity, bias=0.5), "zeros")
    move("s", "pad", T.bf[0:32, :], zeros[0:32, 0:W])
    move("s", "coef", T.coef[:, ::NBIT], zeros[:, 0:TOK // NBIT], "half")
    put("v", "group", lambda: V.tensor_scalar(T.part[:, 1:2], T.part[:, 0:1], GP.bit_length() - 1, None, ALU.arith_shift_right), "p")
    quantise("q zeros", T.pc, T.pz, 0, W, zeros, "zeros")
    scalar_op("m - g", T.turn[:, 0:1], T.part[:, 1:2], -float(GP + 1), T.num[:, 0:1], ALU.mult, ALU.add, "group", "pf")
    quantise("q zeros", T.pc, T.pz, ZEROS[1], ZEROS[1] + W, zeros)
    scalar_op("wrap", T.turn[:, 1:2], T.turn[:, 0:1], 0.0, float(NC), ALU.is_lt, ALU.mult, "m - g")
    quantise("q hp", T.pc, T.pz, W, 2 * W, T.hpt[:, 0:4 * W], "hp")
    scalar_op("window", T.turn[:, 2:3], T.turn[:, 0:1], T.turn[:, 1:2], float(NC - 1), ALU.add, ALU.min, "wrap")
    quantise("q zeros", T.pc, T.pz, ZEROS[2], ZEROS[2] + W, zeros)
    put("v", "start", lambda: V.tensor_scalar(T.turn[:, 4:4 + N], T.num[:, 4:4 + N], T.turn[:, 2:3], None, ALU.mult), "window", "steps")
    quantise(("table", OWN), T.ec, T.ez, 0, K, T.et[:, :], "e")
    for st, (slots, _, _, col, _) in STAGES.items():
        k = len(slots)
        scalar_op(("off", st), T.off[:, col:col + k], T.num[:, 4:4 + k], T.turn[:, 3 + k:4 + k], -1.0, ALU.add, ALU.add, "start")

    def behind(q, word):
        kind, a = word[0], word[1:2]
        if kind in "dp":
            slot, o = int(a), int(word[2])
            at = (slot * O + o) * K
            if kind == "d":
                move(q, ("d", slot, o), T.pr[:, at:at + K], bank_of["m", slot, o][:, 0:K], ("m", slot, o))
            else:
                y, l = (slot_q[slot] * O + o) * TOK, GP * PLACE.index(slot)
                move(q, ("p", slot, o), T.yo[:, y:y + TOK], T.pr[:, at:at + K].indirect(T.li[:, l:l + NC]),
                     ("d", slot, o), ("list", stage_of(slot)))
        elif kind == "w":
            lo, hi = int(a), int(word[2])
            quantise("q qw", T.wc, T.wz, W * lo, W * hi, T.qwt[:, 4 * W * lo:4 * W * hi], word)
            for o in range(lo, hi):
                mark["qw", o] = mark["q qw"]
        elif kind == "x":
            quantise("q x", T.xc, T.xz, 0, TOK, T.xs[:, :], word)
            quantise("q x", T.xc, T.xz, TOK, TOK + W, T.xs[:, 0:4 * W])
        elif kind == "y":
            move(q, "probe", T.probe[:, 0:O * K], T.pr[:, OWN * O * K:N * O * K], *[("d", OWN, o) for o in range(O)])
        elif kind == "z":
            move(q, "probe2", T.probe[:, O * K:2 * O * K], T.pr[:, OWN * O * K:N * O * K], *[("d", OWN, o) for o in range(O)])
        elif kind == "k":
            h, n = int(word[2]), GP * N // 2
            if a == "0":
                move(q, ("bk rows", h), T.bf[0:32, 64 * h:64 * h + n], T.li[0:32, n * h:n * h + n], "pad",
                     *[("list", stage_of(slot)) for slot in PLACE[N // 2 * h:N // 2 * (h + 1)]])
            else:
                put(q, ("bk", h), lambda: V.transpose(T.bt[0:32, 64 * h:64 * h + 64], T.bf[0:32, 64 * h:64 * h + 64]), ("bk rows", h))
        else:
            slots, _, at, col, cuts = STAGES[a]
            k = len(slots)
            step = NBIT * k
            if kind == "b":
                b = int(word[2])
                lo, hi = at + step * cuts[b], at + step * cuts[b + 1]
                scalar_op(("bits", a, b), T.bits[:, lo:hi], bank_of["sg", a, b][:, 0:hi - lo], 0.0, float(K // 2), ALU.is_gt, ALU.mult, ("sg", a, b))
            elif kind == "s":
                b0, b1 = int(word[2]), int(word[3])
                lo, hi = at + step * cuts[b0], at + step * cuts[b1]
                put(q, ("scan", a), lambda: V.tensor_tensor_scan(T.sc[:, lo:hi], T.coef[:, 0:hi - lo], T.bits[:, lo:hi], 0.0, ALU.mult, ALU.add),
                    ("bits", a, b1 - 1), "coef")
            else:
                l = GP * PLACE.index(slots[0])
                move(q, ("list", a), T.li[:, l:l + GP * k], T.sc[:, at:at + step * NC].indirect(T.off[:, col:col + k]),
                     ("scan", a), ("off", a))

    for q, order in (("v", VECTOR), ("s", SCALAR)):
        for word in order.split():
            behind(q, word)

    g.sync.dma_start(T.hpt[:, 0:4 * NBIT], T.hp[:, 0:4 * NBIT]).then_inc(T.sem.ldh, 16)
    g.sync.dma_start(T.et[:, :], T.e[:, :]).then_inc(T.sem.lde, 16)
    for word in LOADS.split():
        if word == "x":
            g.sync.dma_start(T.xs[:, :], T.x[:, :]).then_inc(T.sem.ldx, 16)
        else:
            lo, hi = 4 * W * int(word[1]), 4 * W * int(word[2])
            g.sync.dma_start(T.qwt[:, lo:hi], T.qw[:, lo:hi]).then_inc(T.sem["ld" + word], 16)
    need("y", "q hp")
    for what in "pz":
        g.sync.dma_start(planes(T, GAP, what), planes(T, W + NBIT, what)).then_inc(T.sem.own, 16)

    for q in plan:
        issue(q)

    sent = 0
    for call in CALLS:
        words = call.split()
        need("g", "q hp" if words[0][0] in "pz" else ("table", OWN))
        g.remote_dma_fused([transfer(w[0], w[2:], sets[w[1]], core, T, topo) for w in words], local_sem=T.sem.ls)
        sent += sum(len(sets[w[1]]) for w in words)

    nst = [0]

    def keep(out, in_, *after, q="y"):
        need(q, *after)
        queue[q].dma_start(out, in_).then_inc(T.sem.yst, 16)
        nst[0] += 1

    for word in STORES.split():
        if word[0] == "k":
            h = int(word[1])
            for i, slot in enumerate(PLACE[N // 2 * h:N // 2 * (h + 1)]):
                p, c = GP * (i % 2), 64 * h + 2 * GP * (i // 2)
                keep(T.bk[slot_q[slot], :], T.bt[p:p + NC, c:c + GP], ("bk", h))
        else:
            slot, o0, o1 = (int(ch) for ch in word[-3:])
            y = slot_q[slot] * O * TOK
            keep(T.y[:, y + o0 * TOK:y + o1 * TOK], T.yo[:, y + o0 * TOK:y + o1 * TOK], *[("p", slot, o) for o in range(o0, o1)],
                 q=word[:-3] or "y")

    g.sync.wait_ge(T.sem.yst, 16 * nst[0])
    g.wait_ge(T.sem.ls, sent)
    for q in plan:
        g.wait_ge(T.sem[own_sem[q]], count[q])
